import numpy as np
import ml_dtypes


def mxq(x, axis, fmt="e4m3"):
    dtype, down = {"e4m3": (ml_dtypes.float8_e4m3fn, 7), "e5m2": (ml_dtypes.float8_e5m2, 14)}[fmt]
    v = np.moveaxis(np.asarray(x, np.float32).astype(ml_dtypes.bfloat16).astype(np.float64), axis, -1)
    blocks = v.reshape(v.shape[:-1] + (-1, 32))
    amax = np.abs(blocks).max(-1, keepdims=True)
    byte = np.maximum(np.where(amax > 0, np.frexp(amax)[1] - 1 + 127, 0) - down, 1)
    scale = np.exp2(byte - 127.0)
    codes = (blocks / scale).astype(np.float32).astype(dtype).astype(np.float64)
    return np.moveaxis((codes * scale).reshape(v.shape), -1, axis)


WIDE = False


def mx_kscale(k):
    if not WIDE:
        return np.ones(k)
    levels = np.array([10, -10, 5, -5, 0])
    if k % 512:
        return np.exp2(np.random.permutation(np.resize(levels, k // 32))).repeat(32)
    a = np.empty((k // 512, 16))
    for p in range(k // 512):
        a[p, :8] = np.random.permutation(np.resize(levels, 8))
        for g in range(8):
            far = levels[np.abs(levels - a[p, g]) >= 10]
            a[p, g + 8] = far[np.random.randint(len(far))]
    return np.exp2(a.ravel()).repeat(32)


def f64(x):
    return np.asarray(x).astype(np.float64)


def striped(idx):
    return np.tile(idx.reshape(-1, 16).T, (8, 1)).astype(np.uint16)


def unstriped(offs):
    return offs[:16].T.reshape(-1).astype(np.int64)


def striped8(idx):
    return np.concatenate([x.reshape(-1, 16).T for x in idx]).astype(np.uint16)


def runs(offs, k):
    lists = np.stack([offs[16 * r : 16 * r + 16].T.reshape(-1) for r in range(8)]).astype(np.int64)
    return lists[np.arange(k) % 512 // 64]


def pack_weight(w):
    k, n = w.shape
    w = f64(np.asarray(w, np.float32).astype(ml_dtypes.bfloat16)).reshape(k // 32, 32, n)
    amax = np.abs(w).max(1)
    byte = np.clip(np.where(amax > 0, np.frexp(amax)[1] - 1 + 127 - 7, 1), 1, 254)
    scaled = (w * np.exp2(127.0 - byte)[:, None, :]).reshape(k, n).astype(np.float32)
    words = np.ascontiguousarray(scaled.reshape(k // 512, 128, 4, n).transpose(0, 1, 3, 2)).astype(ml_dtypes.float8_e4m3fn).view(np.uint8)
    return words, np.ascontiguousarray(byte.astype(np.uint8).reshape(k // 512, 16, n))


def unpack_weight(words, scales):
    g, p, n, _ = words.shape
    vals = np.ascontiguousarray(words).view(ml_dtypes.float8_e4m3fn).astype(np.float64) * np.repeat(np.exp2(scales.astype(np.float64) - 127.0), 8, axis=1)[..., None]
    return vals.transpose(0, 1, 3, 2).reshape(g * 512, n)


E2M1 = np.array([0.0, 0.5, 1.0, 1.5, 2.0, 3.0, 4.0, 6.0, -0.0, -0.5, -1.0, -1.5, -2.0, -3.0, -4.0, -6.0])


def pack_fp4(w):
    k, n = w.shape
    w = f64(np.asarray(w, np.float32).astype(ml_dtypes.bfloat16)).reshape(k // 32, 32, n)
    amax = np.abs(w).max(1)
    mant, ex = np.frexp(amax / 6.0)
    byte = np.clip(np.where(amax > 0, np.where(mant > 0.5, ex, ex - 1) + 127, 1), 1, 254)
    scaled = (w * np.exp2(127.0 - byte)[:, None, :]).reshape(k, n).astype(np.float32)
    c = np.ascontiguousarray(scaled.reshape(k // 512, 128, 4, n).transpose(0, 1, 3, 2)).astype(ml_dtypes.float4_e2m1fn).view(np.uint8) & 0xF
    words = (c[..., 0::2] | (c[..., 1::2] << 4)).reshape(k // 512, 128, 2 * n)
    return np.ascontiguousarray(words), np.ascontiguousarray(byte.astype(np.uint8).reshape(k // 512, 16, n))


def unpack_fp4(words, scales):
    g, _, n = scales.shape
    words = np.ascontiguousarray(words).reshape(g, 128, n, 2)
    nib = np.empty((g, 128, n, 4), np.uint8)
    nib[..., 0::2] = words & 0xF
    nib[..., 1::2] = words >> 4
    vals = E2M1[nib] * np.repeat(np.exp2(scales.astype(np.float64) - 127.0), 8, axis=1)[..., None]
    return vals.transpose(0, 1, 3, 2).reshape(g * 512, n)


def planes(y):
    n, m = y.shape
    v = y.astype(np.float32).astype(ml_dtypes.bfloat16).astype(np.float64).reshape(n // 32, 32, m)
    top = np.abs(v).max(1)
    byte = np.clip(np.where(top > 0, np.frexp(top)[1] - 1 + 127 - 7, 1), 1, 254)
    codes = (v * np.exp2(127.0 - byte)[:, None, :]).reshape(n, m).astype(np.float32).astype(ml_dtypes.float8_e4m3fn).view(np.uint8)
    words = codes.reshape(n // 512, 128, 4, m).transpose(0, 1, 3, 2)
    return np.ascontiguousarray(words), np.ascontiguousarray(byte.astype(np.uint8).reshape(n // 512, 16, m))


K, T, S, N, H = 512, 2048, 512, 512, 512


def setup_inputs():
    n = np.random.standard_normal
    s = mx_kscale(K)[:, None]
    u = mx_kscale(S)
    packed_xT = pack_weight(n((K, T)) * s)
    packed_w1 = pack_fp4(n((S, N)) / np.sqrt(S) / u[:, None])
    return {
        "x_words": packed_xT[0],
        "x_scales": packed_xT[1],
        "wa": (n((K, H)) / np.sqrt(K) / s).astype(np.float32),
        "gt": (np.random.uniform(0.5, 1.5, (S, 1)) * u[:, None]).astype(np.float32),
        "w1_words": packed_w1[0],
        "w1_scales": packed_w1[1],
        "offs": striped(np.random.permutation(T)[:S]),
        "n1": striped8(np.stack([np.random.permutation(H) for _ in range(8)])),
        "n2": striped8(np.stack([np.random.permutation(H) for _ in range(8)])),
        "n3": striped8(np.stack([np.random.permutation(H) for _ in range(8)])),
        "n4": striped8(np.stack([np.random.permutation(H) for _ in range(8)])),
    }


def reference(x_words, x_scales, wa, gt, w1_words, w1_scales, offs, n1, n2, n3, n4):
    xq = unpack_weight(x_words, x_scales)[:, unstriped(offs)]
    y = xq.T @ mxq(f64(wa), 0, "e4m3")
    st = y + y[np.arange(S)[:, None], runs(n1, S)]
    z = f64(gt) * (st * (np.tanh(st[np.arange(S)[:, None], runs(n2, S)])))
    h = unpack_fp4(w1_words, w1_scales).T @ mxq(z, 0, "e4m3")
    pa = h[np.arange(N)[:, None], runs(n3, N)]
    pb = h[np.arange(N)[:, None], runs(n4, N)]
    out_0 = np.maximum(np.maximum(h, pa), pb) - (0.5 * (np.minimum(np.minimum(h, pa), pb)))
    return (out_0,) + planes(out_0)

@@ -1,0 +1,170 @@
+from contextlib import ExitStack
+
+import concourse.mybir as mybir
+
+K, T, S, N, H = 512, 2048, 512, 512, 512
+FLOPS = 2 * K * S * H + 2 * S * N * H
+
+F32 = mybir.dt.float32
+BF16 = mybir.dt.bfloat16
+I32 = mybir.dt.int32
+U32 = mybir.dt.uint32
+U16 = mybir.dt.uint16
+U8 = mybir.dt.uint8
+FP8X4 = mybir.dt.float8_e4m3fn_x4
+FP4X4 = mybir.dt.float4_e2m1fn_x4
+ALU = mybir.AluOpType
+ACT = mybir.ActivationFunctionType
+
+P = 128
+PACK = 4
+HALF = H // 2
+
+
+def interleave(engine_copy, dst, src):
+    engine_copy(dst.rearrange("p (c i) t -> p c t i", i=4), src.rearrange("p t (c i) -> p c t i", i=4))
+
+
+def tile_picked_tokhopprange_none_po_kernel(tc, x_words, x_scales, wa, gt, w1_words, w1_scales, offs, n1, n2, n3, n4, out_0, out_1, out_2):
+    nc = tc.nc
+    with ExitStack() as ctx:
+        lists = ctx.enter_context(tc.tile_pool(name="lists", bufs=1))
+        keep = ctx.enter_context(tc.tile_pool(name="keep", bufs=1))
+        psum = ctx.enter_context(tc.psum_pool(name="psum", bufs=1))
+
+        offs_sb = lists.tile([P, S // 16], U16, name="offs_sb")
+        n_sb = [lists.tile([P, H // 16], U16, name="n%d_sb" % i) for i in range(4)]
+
+        warm = keep.tile([P, 8], F32, name="warm")
+        xs_tab = keep.tile([P, T], U8, name="xs_tab", align_bytes=64)
+        xw_tab = keep.tile([P, T], I32, name="xw_tab", align_bytes=64)
+        w1s_raw = keep.tile([P, N], U8, name="w1s_raw", align_bytes=64)
+        w1w_raw = keep.tile([P, 2 * N], U8, name="w1w_raw", align_bytes=64)
+        wa_raw = [keep.tile([P, PACK, HALF], F32, name="wa_raw%d" % u) for u in range(2)]
+        gt_sb = keep.tile([P, PACK], F32, name="gt_sb")
+        rows = [keep.tile([P, 2 * H], F32, name="rows%d" % t, align_bytes=64) for t in range(PACK)]
+        tw = [keep.tile([P, 2 * H], F32, name="tw%d" % t, align_bytes=64) for t in range(PACK)]
+
+        nc.vector.memset(xs_tab[:].bitcast(I32), 0)
+        nc.vector.memset(w1s_raw[:].bitcast(I32), 0)
+        nc.vector.memset(warm[:, 0:4], 0.0)
+        nc.scalar.activation(warm[:, 4:8], warm[:, 0:4], ACT.Tanh)
+        for t in range(PACK):
+            nc.gpsimd.memset(rows[t][:, H:], 0.0)
+
+        nc.sync.dma_start(offs_sb[:], offs)
+        for q in range(4):
+            nc.sync.dma_start(xs_tab[32 * q : 32 * q + 4, :].bitcast(I32), x_scales[0, 4 * q : 4 * q + 4, :].bitcast(I32))
+        nc.sync.dma_start(xw_tab[:], x_words[0].rearrange("p n t -> p (n t)").bitcast(I32))
+        wa_v = wa.rearrange("(p j) c -> p j c", j=PACK)
+        for u in range(2):
+            nc.sync.dma_start(wa_raw[u][:], wa_v[:, :, u * HALF : (u + 1) * HALF])
+        nc.sync.dma_start(w1w_raw[:].bitcast(I32), w1_words[0].bitcast(I32))
+        for q in range(4):
+            nc.sync.dma_start(w1s_raw[32 * q : 32 * q + 4, :].bitcast(I32), w1_scales[0, 4 * q : 4 * q + 4, :].bitcast(I32))
+        nc.sync.dma_start(n_sb[0][:], n1)
+        nc.sync.dma_start(gt_sb[:], gt.rearrange("(p t) o -> p (t o)", t=PACK))
+        nc.sync.dma_start(n_sb[1][:], n2)
+        nc.sync.dma_start(n_sb[2][:], n3)
+        nc.sync.dma_start(n_sb[3][:], n4)
+
+        xs_pick = keep.tile([P, S], U8, name="xs_pick", align_bytes=64)
+        xs = keep.tile([P, S], U8, name="xs", align_bytes=64)
+        xw = keep.tile([P, S], U32, name="xw", align_bytes=64)
+        nc.vector.tensor_copy(xs_pick[:], xs_tab[:].indirect(offs_sb[:]))
+        nc.vector.tensor_copy(xs[:].rearrange("p (t m) -> p t m", t=PACK), xs_pick[:].rearrange("p (m t) -> p t m", t=PACK))
+        nc.vector.tensor_copy(xw[:].rearrange("p (t m) -> p m t", t=PACK), xw_tab[:].bitcast(U32).indirect(offs_sb[:]))
+
+        wa_bf = [keep.tile([P, HALF, PACK], BF16, name="wa_bf%d" % u, align_bytes=64) for u in range(2)]
+        wa_codes = keep.tile([P, H], U32, name="wa_codes", align_bytes=64)
+        wa_sc = keep.tile([P, H], U8, name="wa_sc", align_bytes=64)
+        interleave(nc.scalar.copy, wa_bf[0][:], wa_raw[0][:])
+        interleave(nc.vector.tensor_copy, wa_bf[1][:], wa_raw[1][:])
+        for u in range(2):
+            cols = slice(u * HALF, (u + 1) * HALF)
+            nc.vector.quantize_mx(wa_codes[:, cols].bitcast(FP8X4), wa_sc[:, cols], wa_bf[u][:].rearrange("p c t -> p (c t)"))
+
+        y_ps = [psum.tile([P, H], F32, name="y_ps%d" % t) for t in range(PACK)]
+        for t in range(PACK):
+            m = slice(t * P, (t + 1) * P)
+            nc.tensor.matmul_mx(y_ps[t][:], lhsT=xw[:, m].bitcast(FP8X4), lhsT_scale=xs[:, m], rhs=wa_codes[:].bitcast(FP8X4), rhs_scale=wa_sc[:], start=True, stop=True)
+            nc.scalar.copy(rows[t][:, 0:H], y_ps[t][:])
+
+        w1w = keep.tile([P, 2 * N], U8, name="w1w", align_bytes=64)
+        w1s = keep.tile([P, N], U8, name="w1s", align_bytes=64)
+        nc.vector.tensor_copy(w1w[:].rearrange("p (t m b) -> p t m b", t=PACK, b=2), w1w_raw[:].rearrange("p (m t b) -> p t m b", t=PACK, b=2))
+        nc.vector.tensor_copy(w1s[:].rearrange("p (t m) -> p t m", t=PACK), w1s_raw[:].rearrange("p (m t) -> p t m", t=PACK))
+
+        g1 = [keep.tile([P, H], F32, name="g1_%d" % t) for t in range(PACK)]
+        for t in range(PACK):
+            nc.vector.tensor_copy(g1[t][:], rows[t][:].indirect(n_sb[0][:]))
+            if t > 0:
+                nc.vector.tensor_tensor(tw[t - 1][:, H:], g1[t - 1][:], y_ps[t - 1][:], ALU.add)
+                nc.scalar.activation(tw[t - 1][:, 0:H], tw[t - 1][:, H:], ACT.Tanh)
+        t = PACK - 1
+        nc.vector.tensor_tensor(tw[t][:, H:], g1[t][:], y_ps[t][:], ALU.add)
+        nc.scalar.activation(tw[t][:, 0:H], tw[t][:, H:], ACT.Tanh)
+
+        g2 = [keep.tile([P, PACK, HALF], F32, name="g2_%d" % u) for u in range(2)]
+        z = [keep.tile([P, PACK, HALF], F32, name="z%d" % u) for u in range(2)]
+        z_bf = [keep.tile([P, HALF, PACK], BF16, name="z_bf%d" % u, align_bytes=64) for u in range(2)]
+        z_codes = [keep.tile([P, HALF], U32, name="z_codes%d" % u, align_bytes=64) for u in range(2)]
+        z_sc = [keep.tile([P, HALF], U8, name="z_sc%d" % u, align_bytes=64) for u in range(2)]
+        h_ps = [psum.tile([P, H], F32, name="h_ps%d" % t) for t in range(PACK)]
+        for u in range(2):
+            lo = u * HALF
+            for t in range(PACK + 1):
+                if t < PACK:
+                    nc.vector.tensor_copy(g2[u][:, t, :], tw[t][:].indirect(n_sb[1][:, lo // 16 : (lo + HALF) // 16]))
+                if t > 0:
+                    s = t - 1
+                    nc.vector.scalar_tensor_tensor(z[u][:, s, :], g2[u][:, s, :], gt_sb[:, s : s + 1], tw[s][:, H + lo : H + lo + HALF], ALU.mult, ALU.mult)
+            if u == 0:
+                interleave(nc.scalar.copy, z_bf[u][:], z[u][:])
+            else:
+                interleave(nc.scalar.copy, z_bf[u][:, 0:96, :], z[u][:, :, 0:96])
+                interleave(nc.vector.tensor_copy, z_bf[u][:, 96:, :], z[u][:, :, 96:])
+            nc.vector.quantize_mx(z_codes[u][:].bitcast(FP8X4), z_sc[u][:], z_bf[u][:].rearrange("p c t -> p (c t)"))
+            for t in range(PACK):
+                nc.tensor.matmul_mx(h_ps[t][:, lo : lo + HALF], lhsT=w1w[:, 2 * P * t : 2 * P * (t + 1)].bitcast(FP4X4), lhsT_scale=w1s[:, t * P : (t + 1) * P], rhs=z_codes[u][:].bitcast(FP8X4), rhs_scale=z_sc[u][:], start=True, stop=True)
+                nc.scalar.copy(rows[t][:, lo : lo + HALF], h_ps[t][:, lo : lo + HALF])
+
+        o_codes = keep.tile([P, H], I32, name="o_codes", align_bytes=64)
+        o_sc = keep.tile([P, H], U8, name="o_sc", align_bytes=64)
+        out_v = out_0.rearrange("(p t) c -> p t c", t=PACK)
+        words_v = out_1[0].rearrange("p n t -> p (n t)").bitcast(I32)
+        for u in range(2):
+            lo = u * HALF
+            cols = slice(lo, lo + HALF)
+            ents = slice(lo // 16, (lo + HALF) // 16)
+            pa = keep.tile([P, PACK, HALF], F32, name="pa%d" % u)
+            pb = keep.tile([P, PACK, HALF], F32, name="pb%d" % u)
+            hi = keep.tile([P, PACK, HALF], F32, name="hi%d" % u)
+            lw = keep.tile([P, PACK, HALF], F32, name="lw%d" % u)
+            hi2 = keep.tile([P, PACK, HALF], F32, name="hi2_%d" % u)
+            lw2 = keep.tile([P, PACK, HALF], F32, name="lw2_%d" % u)
+            o = keep.tile([P, PACK, HALF], F32, name="o%d" % u)
+            o_bf = keep.tile([P, HALF, PACK], BF16, name="o_bf%d" % u, align_bytes=64)
+            for t in range(PACK):
+                nc.vector.tensor_copy(pa[:, t, :], rows[t][:].indirect(n_sb[2][:, ents]))
+                nc.vector.tensor_copy(pb[:, t, :], rows[t][:].indirect(n_sb[3][:, ents]))
+                nc.vector.tensor_tensor(hi[:, t, :], pa[:, t, :], rows[t][:, cols], ALU.max)
+                nc.vector.tensor_tensor(lw[:, t, :], pa[:, t, :], rows[t][:, cols], ALU.min)
+            for a in range(2):
+                pr = slice(2 * a, 2 * a + 2)
+                nc.vector.tensor_tensor(lw2[:, pr, :], lw[:, pr, :], pb[:, pr, :], ALU.min)
+                nc.vector.tensor_tensor(hi2[:, pr, :], hi[:, pr, :], pb[:, pr, :], ALU.max)
+            for a in range(2):
+                pr = slice(2 * a, 2 * a + 2)
+                nc.vector.scalar_tensor_tensor(o[:, pr, :], lw2[:, pr, :], -0.5, hi2[:, pr, :], ALU.mult, ALU.add)
+                nc.sync.dma_start(out_v[:, pr, cols], o[:, pr, :])
+            if u == 0:
+                interleave(nc.scalar.copy, o_bf[:], o[:])
+            else:
+                interleave(nc.scalar.copy, o_bf[:, 0:96, :], o[:, :, 0:96])
+                interleave(nc.vector.tensor_copy, o_bf[:, 96:, :], o[:, :, 96:])
+            nc.vector.quantize_mx(o_codes[:, cols].bitcast(FP8X4), o_sc[:, cols], o_bf[:].rearrange("p c t -> p (c t)"))
+            nc.sync.dma_start(words_v[:, cols], o_codes[:, cols])
+        for q in range(4):
+            eng = nc.scalar if q % 2 == 0 else nc.sync
+            eng.dma_start(out_2[0, 4 * q : 4 * q + 4, :].bitcast(I32), o_sc[32 * q : 32 * q + 4, :].bitcast(I32))

@@ -84,41 +84,35 @@ def tile_picked_tokhopprange_none_po_kernel(tc, x_words, x_scales, wa, gt, w1_wo
             cols = slice(u * HALF, (u + 1) * HALF)
             nc.vector.quantize_mx(wa_codes[:, cols].bitcast(FP8X4), wa_sc[:, cols], wa_bf[u][:].rearrange("p c t -> p (c t)"))
 
+        plain = [keep.tile([P, H], F32, name="plain%d" % t) for t in range(PACK)]
+        stg = [keep.tile([P, H], F32, name="stg%d" % t) for t in range(PACK)]
         y_ps = [psum.tile([P, H], F32, name="y_ps%d" % t) for t in range(PACK)]
         for t in range(PACK):
             m = slice(t * P, (t + 1) * P)
             nc.tensor.matmul_mx(y_ps[t][:], lhsT=xw[:, m].bitcast(FP8X4), lhsT_scale=xs[:, m], rhs=wa_codes[:].bitcast(FP8X4), rhs_scale=wa_sc[:], start=True, stop=True)
             nc.scalar.copy(rows[t][:, 0:H], y_ps[t][:])
+            nc.scalar.copy(plain[t][:], y_ps[t][:])
 
         w1w = keep.tile([P, 2 * N], U8, name="w1w", align_bytes=64)
         w1s = keep.tile([P, N], U8, name="w1s", align_bytes=64)
         nc.vector.tensor_copy(w1w[:].rearrange("p (t m b) -> p t m b", t=PACK, b=2), w1w_raw[:].rearrange("p (m t b) -> p t m b", t=PACK, b=2))
         nc.vector.tensor_copy(w1s[:].rearrange("p (t m) -> p t m", t=PACK), w1s_raw[:].rearrange("p (m t) -> p t m", t=PACK))
 
-        g1 = [keep.tile([P, H], F32, name="g1_%d" % t) for t in range(PACK)]
         for t in range(PACK):
-            nc.vector.tensor_copy(g1[t][:], rows[t][:].indirect(n_sb[0][:]))
-            if t > 0:
-                nc.vector.tensor_tensor(tw[t - 1][:, H:], g1[t - 1][:], y_ps[t - 1][:], ALU.add)
-                nc.scalar.activation(tw[t - 1][:, 0:H], tw[t - 1][:, H:], ACT.Tanh)
-        t = PACK - 1
-        nc.vector.tensor_tensor(tw[t][:, H:], g1[t][:], y_ps[t][:], ALU.add)
-        nc.scalar.activation(tw[t][:, 0:H], tw[t][:, H:], ACT.Tanh)
+            nc.vector.tensor_tensor(tw[t][:, H:], rows[t][:].indirect(n_sb[0][:]), plain[t][:], ALU.add)
+            nc.scalar.activation(tw[t][:, 0:H], tw[t][:, H:], ACT.Tanh)
+            nc.scalar.activation(stg[t][:], tw[t][:, H:], ACT.Copy, scale=gt_sb[:, t : t + 1])
 
-        g2 = [keep.tile([P, PACK, HALF], F32, name="g2_%d" % u) for u in range(2)]
         z = [keep.tile([P, PACK, HALF], F32, name="z%d" % u) for u in range(2)]
         z_bf = [keep.tile([P, HALF, PACK], BF16, name="z_bf%d" % u, align_bytes=64) for u in range(2)]
         z_codes = [keep.tile([P, HALF], U32, name="z_codes%d" % u, align_bytes=64) for u in range(2)]
         z_sc = [keep.tile([P, HALF], U8, name="z_sc%d" % u, align_bytes=64) for u in range(2)]
+        hp = [keep.tile([P, PACK, HALF], F32, name="hp%d" % u) for u in range(2)]
         h_ps = [psum.tile([P, H], F32, name="h_ps%d" % t) for t in range(PACK)]
         for u in range(2):
             lo = u * HALF
-            for t in range(PACK + 1):
-                if t < PACK:
-                    nc.vector.tensor_copy(g2[u][:, t, :], tw[t][:].indirect(n_sb[1][:, lo // 16 : (lo + HALF) // 16]))
-                if t > 0:
-                    s = t - 1
-                    nc.vector.scalar_tensor_tensor(z[u][:, s, :], g2[u][:, s, :], gt_sb[:, s : s + 1], tw[s][:, H + lo : H + lo + HALF], ALU.mult, ALU.mult)
+            for t in range(PACK):
+                nc.vector.tensor_tensor(z[u][:, t, :], tw[t][:].indirect(n_sb[1][:, lo // 16 : (lo + HALF) // 16]), stg[t][:, lo : lo + HALF], ALU.mult)
             if u == 0:
                 interleave(nc.scalar.copy, z_bf[u][:], z[u][:])
             else:
@@ -128,6 +122,8 @@ def tile_picked_tokhopprange_none_po_kernel(tc, x_words, x_scales, wa, gt, w1_wo
             for t in range(PACK):
                 nc.tensor.matmul_mx(h_ps[t][:, lo : lo + HALF], lhsT=w1w[:, 2 * P * t : 2 * P * (t + 1)].bitcast(FP4X4), lhsT_scale=w1s[:, t * P : (t + 1) * P], rhs=z_codes[u][:].bitcast(FP8X4), rhs_scale=z_sc[u][:], start=True, stop=True)
                 nc.scalar.copy(rows[t][:, lo : lo + HALF], h_ps[t][:, lo : lo + HALF])
+            for t in range(PACK):
+                nc.scalar.copy(hp[u][:, t, :], h_ps[t][:, lo : lo + HALF])
 
         o_codes = keep.tile([P, H], I32, name="o_codes", align_bytes=64)
         o_sc = keep.tile([P, H], U8, name="o_sc", align_bytes=64)
@@ -142,21 +138,21 @@ def tile_picked_tokhopprange_none_po_kernel(tc, x_words, x_scales, wa, gt, w1_wo
             hi = keep.tile([P, PACK, HALF], F32, name="hi%d" % u)
             lw = keep.tile([P, PACK, HALF], F32, name="lw%d" % u)
             hi2 = keep.tile([P, PACK, HALF], F32, name="hi2_%d" % u)
-            lw2 = keep.tile([P, PACK, HALF], F32, name="lw2_%d" % u)
             o = keep.tile([P, PACK, HALF], F32, name="o%d" % u)
             o_bf = keep.tile([P, HALF, PACK], BF16, name="o_bf%d" % u, align_bytes=64)
             for t in range(PACK):
-                nc.vector.tensor_copy(pa[:, t, :], rows[t][:].indirect(n_sb[2][:, ents]))
-                nc.vector.tensor_copy(pb[:, t, :], rows[t][:].indirect(n_sb[3][:, ents]))
-                nc.vector.tensor_tensor(hi[:, t, :], pa[:, t, :], rows[t][:, cols], ALU.max)
-                nc.vector.tensor_tensor(lw[:, t, :], pa[:, t, :], rows[t][:, cols], ALU.min)
+                nc.vector.tensor_tensor(pa[:, t, :], rows[t][:].indirect(n_sb[2][:, ents]), hp[u][:, t, :], ALU.subtract)
+                nc.vector.tensor_tensor(pb[:, t, :], rows[t][:].indirect(n_sb[3][:, ents]), hp[u][:, t, :], ALU.subtract)
             for a in range(2):
                 pr = slice(2 * a, 2 * a + 2)
-                nc.vector.tensor_tensor(lw2[:, pr, :], lw[:, pr, :], pb[:, pr, :], ALU.min)
-                nc.vector.tensor_tensor(hi2[:, pr, :], hi[:, pr, :], pb[:, pr, :], ALU.max)
+                nc.vector.scalar_tensor_tensor(lw[:, pr, :], pa[:, pr, :], 0.0, pb[:, pr, :], ALU.min, ALU.min)
+                nc.vector.scalar_tensor_tensor(hi[:, pr, :], pa[:, pr, :], 0.0, pb[:, pr, :], ALU.max, ALU.max)
             for a in range(2):
                 pr = slice(2 * a, 2 * a + 2)
-                nc.vector.scalar_tensor_tensor(o[:, pr, :], lw2[:, pr, :], -0.5, hi2[:, pr, :], ALU.mult, ALU.add)
+                nc.vector.scalar_tensor_tensor(hi2[:, pr, :], lw[:, pr, :], -0.5, hi[:, pr, :], ALU.mult, ALU.add)
+            for a in range(2):
+                pr = slice(2 * a, 2 * a + 2)
+                nc.vector.scalar_tensor_tensor(o[:, pr, :], hp[u][:, pr, :], 0.5, hi2[:, pr, :], ALU.mult, ALU.add)
                 nc.sync.dma_start(out_v[:, pr, cols], o[:, pr, :])
             if u == 0:
                 interleave(nc.scalar.copy, o_bf[:], o[:])

@@ -1,6 +1,7 @@
 from contextlib import ExitStack
 
 import concourse.mybir as mybir
+from concourse.masks import make_identity
 
 K, T, S, N, H = 512, 2048, 512, 512, 512
 FLOPS = 2 * K * S * H + 2 * S * N * H
@@ -25,6 +26,10 @@ def interleave(engine_copy, dst, src):
     engine_copy(dst.rearrange("p (c i) t -> p c t i", i=4), src.rearrange("p t (c i) -> p c t i", i=4))
 
 
+def entries(offsets, lo, width):
+    return offsets[:, lo // 16 : (lo + width) // 16]
+
+
 def tile_picked_tokhopprange_none_po_kernel(tc, x_words, x_scales, wa, gt, w1_words, w1_scales, offs, n1, n2, n3, n4, out_0, out_1, out_2):
     nc = tc.nc
     with ExitStack() as ctx:
@@ -33,134 +38,200 @@ def tile_picked_tokhopprange_none_po_kernel(tc, x_words, x_scales, wa, gt, w1_wo
         psum = ctx.enter_context(tc.psum_pool(name="psum", bufs=1))
 
         offs_sb = lists.tile([P, S // 16], U16, name="offs_sb")
-        n_sb = [lists.tile([P, H // 16], U16, name="n%d_sb" % i) for i in range(4)]
+        n1_sb = lists.tile([P, H // 16], U16, name="n1_sb")
+        n2_sb = lists.tile([P, H // 16], U16, name="n2_sb")
+        n3_sb = lists.tile([P, H // 16], U16, name="n3_sb")
+        n4_sb = lists.tile([P, H // 16], U16, name="n4_sb")
+        bank = [psum.tile([P, H], F32, name="bank%d" % b) for b in range(8)]
 
-        warm = keep.tile([P, 8], F32, name="warm")
-        xs_tab = keep.tile([P, T], U8, name="xs_tab", align_bytes=64)
-        xw_tab = keep.tile([P, T], I32, name="xw_tab", align_bytes=64)
-        w1s_raw = keep.tile([P, N], U8, name="w1s_raw", align_bytes=64)
-        w1w_raw = keep.tile([P, 2 * N], U8, name="w1w_raw", align_bytes=64)
-        wa_raw = [keep.tile([P, PACK, HALF], F32, name="wa_raw%d" % u) for u in range(2)]
+        ident = keep.tile([P, P], F32, name="ident")
+        xs_tab = keep.tile([P, T], U8, name="xs_tab", tag="xs_place", align_bytes=64)
+        wa_raw = keep.tile([P, PACK, H], F32, name="wa_raw")
         gt_sb = keep.tile([P, PACK], F32, name="gt_sb")
-        rows = [keep.tile([P, 2 * H], F32, name="rows%d" % t, align_bytes=64) for t in range(PACK)]
-        tw = [keep.tile([P, 2 * H], F32, name="tw%d" % t, align_bytes=64) for t in range(PACK)]
+        y_win = [keep.tile([P, 2 * H], F32, name="y_win%d" % t, align_bytes=64) for t in range(PACK)]
+        warm = keep.tile([P, 8], F32, name="warm", tag="x_place", align_bytes=64)
 
+        nc.sync.dma_start(offs_sb[:], offs)
+        nc.sync.dma_start(gt_sb[:], gt.rearrange("(p t) o -> p (t o)", t=PACK))
         nc.vector.memset(xs_tab[:].bitcast(I32), 0)
-        nc.vector.memset(w1s_raw[:].bitcast(I32), 0)
         nc.vector.memset(warm[:, 0:4], 0.0)
         nc.scalar.activation(warm[:, 4:8], warm[:, 0:4], ACT.Tanh)
         for t in range(PACK):
-            nc.gpsimd.memset(rows[t][:, H:], 0.0)
+            nc.vector.memset(y_win[t][:, H:], 0.0)
+        th_win = [keep.tile([P, 2 * H if t == PACK - 1 else H], F32, name="th_win%d" % t, align_bytes=64) for t in range(PACK)]
+        nc.vector.memset(th_win[PACK - 1][:, H:], 0.0)
+        make_identity(nc, ident[:])
 
-        nc.sync.dma_start(offs_sb[:], offs)
+        gt_safe = keep.tile([P, PACK], F32, name="gt_safe", tag="w1w_place", align_bytes=64)
+        gt_rec = keep.tile([P, PACK], F32, name="gt_rec", tag="w1s_place", align_bytes=64)
+        gt_inv = keep.tile([P, PACK], F32, name="gt_inv")
+        nc.vector.scalar_tensor_tensor(gt_safe[:], gt_sb[:], 0.0, gt_sb[:], ALU.is_equal, ALU.add)
+        nc.vector.reciprocal(gt_rec[:], gt_safe[:])
+        nc.vector.tensor_scalar(gt_inv[:], gt_rec[:], 1.0e38, -1.0e38, ALU.min, ALU.max)
+
+        xw_tab = keep.tile([P, T], I32, name="xw_tab", tag="x_place", align_bytes=64)
+        w1w_raw = keep.tile([P, 2 * N], U8, name="w1w_raw", tag="w1w_place", align_bytes=64)
+        w1s_raw = keep.tile([P, N], U8, name="w1s_raw", tag="w1s_place", align_bytes=64)
+        nc.vector.memset(w1s_raw[:].bitcast(I32), 0)
+
+        nc.sync.dma_start(n1_sb[:], n1)
+        nc.sync.dma_start(n2_sb[:], n2)
+        nc.sync.dma_start(wa_raw[:], wa.rearrange("(p j) c -> p j c", j=PACK))
         for q in range(4):
             nc.sync.dma_start(xs_tab[32 * q : 32 * q + 4, :].bitcast(I32), x_scales[0, 4 * q : 4 * q + 4, :].bitcast(I32))
         nc.sync.dma_start(xw_tab[:], x_words[0].rearrange("p n t -> p (n t)").bitcast(I32))
-        wa_v = wa.rearrange("(p j) c -> p j c", j=PACK)
-        for u in range(2):
-            nc.sync.dma_start(wa_raw[u][:], wa_v[:, :, u * HALF : (u + 1) * HALF])
+        nc.sync.dma_start(n3_sb[:], n3)
+        nc.sync.dma_start(n4_sb[:], n4)
         nc.sync.dma_start(w1w_raw[:].bitcast(I32), w1_words[0].bitcast(I32))
         for q in range(4):
             nc.sync.dma_start(w1s_raw[32 * q : 32 * q + 4, :].bitcast(I32), w1_scales[0, 4 * q : 4 * q + 4, :].bitcast(I32))
-        nc.sync.dma_start(n_sb[0][:], n1)
-        nc.sync.dma_start(gt_sb[:], gt.rearrange("(p t) o -> p (t o)", t=PACK))
-        nc.sync.dma_start(n_sb[1][:], n2)
-        nc.sync.dma_start(n_sb[2][:], n3)
-        nc.sync.dma_start(n_sb[3][:], n4)
-
-        xs_pick = keep.tile([P, S], U8, name="xs_pick", align_bytes=64)
-        xs = keep.tile([P, S], U8, name="xs", align_bytes=64)
-        xw = keep.tile([P, S], U32, name="xw", align_bytes=64)
-        nc.vector.tensor_copy(xs_pick[:], xs_tab[:].indirect(offs_sb[:]))
-        nc.vector.tensor_copy(xs[:].rearrange("p (t m) -> p t m", t=PACK), xs_pick[:].rearrange("p (m t) -> p t m", t=PACK))
-        nc.vector.tensor_copy(xw[:].rearrange("p (t m) -> p m t", t=PACK), xw_tab[:].bitcast(U32).indirect(offs_sb[:]))
 
         wa_bf = [keep.tile([P, HALF, PACK], BF16, name="wa_bf%d" % u, align_bytes=64) for u in range(2)]
         wa_codes = keep.tile([P, H], U32, name="wa_codes", align_bytes=64)
-        wa_sc = keep.tile([P, H], U8, name="wa_sc", align_bytes=64)
-        interleave(nc.scalar.copy, wa_bf[0][:], wa_raw[0][:])
-        interleave(nc.vector.tensor_copy, wa_bf[1][:], wa_raw[1][:])
-        for u in range(2):
-            cols = slice(u * HALF, (u + 1) * HALF)
-            nc.vector.quantize_mx(wa_codes[:, cols].bitcast(FP8X4), wa_sc[:, cols], wa_bf[u][:].rearrange("p c t -> p (c t)"))
+        xs_pick = keep.tile([P, S], U8, name="xs_pick", tag="xw_place", align_bytes=64)
+        xs = keep.tile([P, S], U8, name="xs", align_bytes=64)
+        halves = [slice(0, HALF), slice(HALF, H)]
+        interleave(nc.vector.tensor_copy, wa_bf[1][:, HALF - 128 :, :], wa_raw[:, :, H - 128 :])
+        interleave(nc.scalar.copy, wa_bf[0][:], wa_raw[:, :, halves[0]])
+        interleave(nc.scalar.copy, wa_bf[1][:, 0 : HALF - 128, :], wa_raw[:, :, HALF : H - 128])
+        nc.vector.tensor_copy(xs_pick[:], xs_tab[:].indirect(offs_sb[:]))
+        wa_sc = keep.tile([P, H], U8, name="wa_sc", tag="xs_place", align_bytes=64)
+        nc.vector.quantize_mx(wa_codes[:, halves[0]].bitcast(FP8X4), wa_sc[:, halves[0]], wa_bf[0][:].rearrange("p c t -> p (c t)"))
+        nc.vector.tensor_copy(xs[:].rearrange("p (t m) -> p t m", t=PACK), xs_pick[:].rearrange("p (m t) -> p t m", t=PACK))
+        xw = keep.tile([P, S], U32, name="xw", tag="xw_place", align_bytes=64)
+        nc.vector.tensor_copy(xw[:].rearrange("p (t m) -> p m t", t=PACK), xw_tab[:].bitcast(U32).indirect(offs_sb[:]))
+        nc.vector.quantize_mx(wa_codes[:, halves[1]].bitcast(FP8X4), wa_sc[:, halves[1]], wa_bf[1][:].rearrange("p c t -> p (c t)"))
 
-        plain = [keep.tile([P, H], F32, name="plain%d" % t) for t in range(PACK)]
-        stg = [keep.tile([P, H], F32, name="stg%d" % t) for t in range(PACK)]
-        y_ps = [psum.tile([P, H], F32, name="y_ps%d" % t) for t in range(PACK)]
+        y_plain = [keep.tile([P, H], F32, name="y_plain%d" % t) for t in range(PACK)]
         for t in range(PACK):
             m = slice(t * P, (t + 1) * P)
-            nc.tensor.matmul_mx(y_ps[t][:], lhsT=xw[:, m].bitcast(FP8X4), lhsT_scale=xs[:, m], rhs=wa_codes[:].bitcast(FP8X4), rhs_scale=wa_sc[:], start=True, stop=True)
-            nc.scalar.copy(rows[t][:, 0:H], y_ps[t][:])
-            nc.scalar.copy(plain[t][:], y_ps[t][:])
+            g = gt_sb[:, t : t + 1]
+            if t == 0:
+                for u in range(2):
+                    cols = slice(u * HALF, (u + 1) * HALF)
+                    nc.tensor.matmul_mx(bank[4 * u][:, 0:HALF], lhsT=xw[:, m].bitcast(FP8X4), lhsT_scale=xs[:, m], rhs=wa_codes[:, cols].bitcast(FP8X4), rhs_scale=wa_sc[:, cols], start=True, stop=True)
+                nc.scalar.activation(y_win[t][:, 0:HALF], bank[0][:, 0:HALF], ACT.Copy, scale=g)
+                nc.scalar.activation(y_win[t][:, HALF:H], bank[4][:, 0:HALF], ACT.Copy, scale=g)
+                nc.vector.tensor_scalar(y_plain[t][:, 0:HALF], bank[0][:, 0:HALF], g, None, ALU.mult)
+                nc.scalar.activation(y_plain[t][:, HALF:H], bank[4][:, 0:HALF], ACT.Copy, scale=g)
+            else:
+                nc.tensor.matmul_mx(bank[t][:], lhsT=xw[:, m].bitcast(FP8X4), lhsT_scale=xs[:, m], rhs=wa_codes[:].bitcast(FP8X4), rhs_scale=wa_sc[:], start=True, stop=True)
+                nc.scalar.activation(y_win[t][:, 0:H], bank[t][:], ACT.Copy, scale=g)
+                nc.scalar.activation(y_plain[t][:], bank[t][:], ACT.Copy, scale=g)
 
-        w1w = keep.tile([P, 2 * N], U8, name="w1w", align_bytes=64)
-        w1s = keep.tile([P, N], U8, name="w1s", align_bytes=64)
+        w1w = keep.tile([P, 2 * N], U8, name="w1w", tag="x_place", align_bytes=64)
+        w1s = keep.tile([P, N], U8, name="w1s", tag="w1w_place", align_bytes=64)
         nc.vector.tensor_copy(w1w[:].rearrange("p (t m b) -> p t m b", t=PACK, b=2), w1w_raw[:].rearrange("p (m t b) -> p t m b", t=PACK, b=2))
         nc.vector.tensor_copy(w1s[:].rearrange("p (t m) -> p t m", t=PACK), w1s_raw[:].rearrange("p (m t) -> p t m", t=PACK))
 
+        stg = keep.tile([P, PACK, H], F32, name="stg")
         for t in range(PACK):
-            nc.vector.tensor_tensor(tw[t][:, H:], rows[t][:].indirect(n_sb[0][:]), plain[t][:], ALU.add)
-            nc.scalar.activation(tw[t][:, 0:H], tw[t][:, H:], ACT.Tanh)
-            nc.scalar.activation(stg[t][:], tw[t][:, H:], ACT.Copy, scale=gt_sb[:, t : t + 1])
+            nc.vector.tensor_tensor(stg[:, PACK - 1 - t, :], y_win[t][:].indirect(n1_sb[:]), y_plain[t][:], ALU.add)
+            nc.scalar.activation(th_win[t][:, 0:H], stg[:, PACK - 1 - t, :], ACT.Tanh, scale=gt_inv[:, t : t + 1])
 
-        z = [keep.tile([P, PACK, HALF], F32, name="z%d" % u) for u in range(2)]
+        h_win = [keep.tile([P, H], F32, name="h_win%d" % t, align_bytes=64) for t in range(PACK)]
+        h_neg = [keep.tile([P, PACK, HALF], F32, name="h_neg%d" % u) for u in range(2)]
+        z_left = keep.tile([P, PACK, HALF], F32, name="z_left")
+        z_pair = [th_win[PACK - 1][:, H:].rearrange("p (t c) -> p t c", t=2), stg[:, 0:2, 0:HALF]]
         z_bf = [keep.tile([P, HALF, PACK], BF16, name="z_bf%d" % u, align_bytes=64) for u in range(2)]
         z_codes = [keep.tile([P, HALF], U32, name="z_codes%d" % u, align_bytes=64) for u in range(2)]
         z_sc = [keep.tile([P, HALF], U8, name="z_sc%d" % u, align_bytes=64) for u in range(2)]
-        hp = [keep.tile([P, PACK, HALF], F32, name="hp%d" % u) for u in range(2)]
-        h_ps = [psum.tile([P, H], F32, name="h_ps%d" % t) for t in range(PACK)]
-        for u in range(2):
-            lo = u * HALF
-            for t in range(PACK):
-                nc.vector.tensor_tensor(z[u][:, t, :], tw[t][:].indirect(n_sb[1][:, lo // 16 : (lo + HALF) // 16]), stg[t][:, lo : lo + HALF], ALU.mult)
-            if u == 0:
-                interleave(nc.scalar.copy, z_bf[u][:], z[u][:])
-            else:
-                interleave(nc.scalar.copy, z_bf[u][:, 0:96, :], z[u][:, :, 0:96])
-                interleave(nc.vector.tensor_copy, z_bf[u][:, 96:, :], z[u][:, :, 96:])
-            nc.vector.quantize_mx(z_codes[u][:].bitcast(FP8X4), z_sc[u][:], z_bf[u][:].rearrange("p c t -> p (c t)"))
-            for t in range(PACK):
-                nc.tensor.matmul_mx(h_ps[t][:, lo : lo + HALF], lhsT=w1w[:, 2 * P * t : 2 * P * (t + 1)].bitcast(FP4X4), lhsT_scale=w1s[:, t * P : (t + 1) * P], rhs=z_codes[u][:].bitcast(FP8X4), rhs_scale=z_sc[u][:], start=True, stop=True)
-                nc.scalar.copy(rows[t][:, lo : lo + HALF], h_ps[t][:, lo : lo + HALF])
-            for t in range(PACK):
-                nc.scalar.copy(hp[u][:, t, :], h_ps[t][:, lo : lo + HALF])
+        quarters = [slice(0, P), slice(P, HALF)]
+        for t in range(PACK):
+            nc.vector.tensor_tensor(z_left[:, t, :], th_win[t][:].indirect(entries(n2_sb, 0, HALF)), stg[:, PACK - 1 - t, 0:HALF], ALU.mult)
+        interleave(nc.scalar.copy, z_bf[0][:], z_left[:])
+        for t in range(PACK):
+            nc.vector.tensor_tensor(z_pair[t // 2][:, t % 2, :], th_win[t][:].indirect(entries(n2_sb, HALF, HALF)), stg[:, PACK - 1 - t, HALF:], ALU.mult)
+        nc.scalar.copy(z_bf[1][:, :, 0:2], z_pair[0].rearrange("p t c -> p c t"))
+        nc.vector.quantize_mx(z_codes[0][:].bitcast(FP8X4), z_sc[0][:], z_bf[0][:].rearrange("p c t -> p (c t)"))
+        for c in quarters:
+            nc.vector.tensor_copy(z_bf[1][:, c, 2:4], z_pair[1][:, :, c].rearrange("p t c -> p c t"))
+        for c in quarters:
+            nc.vector.quantize_mx(z_codes[1][:, c].bitcast(FP8X4), z_sc[1][:, c], z_bf[1][:, c, :].rearrange("p c t -> p (c t)"))
+
+        def second_product(t, u, c):
+            nc.tensor.matmul_mx(bank[PACK * u + t][:, c], lhsT=w1w[:, 2 * P * t : 2 * P * (t + 1)].bitcast(FP4X4), lhsT_scale=w1s[:, t * P : (t + 1) * P], rhs=z_codes[u][:, c].bitcast(FP8X4), rhs_scale=z_sc[u][:, c], start=True, stop=True)
+
+        for t in range(PACK):
+            second_product(t, 0, slice(0, HALF))
+            for c in quarters if t == 0 else [slice(0, HALF)]:
+                second_product(t, 1, c)
+            nc.scalar.copy(h_win[t][:, 0:HALF], bank[t][:, 0:HALF])
+            nc.scalar.activation(h_neg[0][:, t, :], bank[t][:, 0:HALF], ACT.Copy, scale=-1.0)
+            nc.scalar.copy(h_win[t][:, HALF:H], bank[PACK + t][:, 0:HALF])
+        for t in range(PACK):
+            nc.scalar.activation(h_neg[1][:, t, :], bank[PACK + t][:, 0:HALF], ACT.Copy, scale=-1.0)
 
         o_codes = keep.tile([P, H], I32, name="o_codes", align_bytes=64)
         o_sc = keep.tile([P, H], U8, name="o_sc", align_bytes=64)
         out_v = out_0.rearrange("(p t) c -> p t c", t=PACK)
         words_v = out_1[0].rearrange("p n t -> p (n t)").bitcast(I32)
-        for u in range(2):
-            lo = u * HALF
-            cols = slice(lo, lo + HALF)
-            ents = slice(lo // 16, (lo + HALF) // 16)
-            pa = keep.tile([P, PACK, HALF], F32, name="pa%d" % u)
-            pb = keep.tile([P, PACK, HALF], F32, name="pb%d" % u)
-            hi = keep.tile([P, PACK, HALF], F32, name="hi%d" % u)
-            lw = keep.tile([P, PACK, HALF], F32, name="lw%d" % u)
-            hi2 = keep.tile([P, PACK, HALF], F32, name="hi2_%d" % u)
-            o = keep.tile([P, PACK, HALF], F32, name="o%d" % u)
-            o_bf = keep.tile([P, HALF, PACK], BF16, name="o_bf%d" % u, align_bytes=64)
-            for t in range(PACK):
-                nc.vector.tensor_tensor(pa[:, t, :], rows[t][:].indirect(n_sb[2][:, ents]), hp[u][:, t, :], ALU.subtract)
-                nc.vector.tensor_tensor(pb[:, t, :], rows[t][:].indirect(n_sb[3][:, ents]), hp[u][:, t, :], ALU.subtract)
-            for a in range(2):
-                pr = slice(2 * a, 2 * a + 2)
-                nc.vector.scalar_tensor_tensor(lw[:, pr, :], pa[:, pr, :], 0.0, pb[:, pr, :], ALU.min, ALU.min)
-                nc.vector.scalar_tensor_tensor(hi[:, pr, :], pa[:, pr, :], 0.0, pb[:, pr, :], ALU.max, ALU.max)
-            for a in range(2):
-                pr = slice(2 * a, 2 * a + 2)
-                nc.vector.scalar_tensor_tensor(hi2[:, pr, :], lw[:, pr, :], -0.5, hi[:, pr, :], ALU.mult, ALU.add)
-            for a in range(2):
-                pr = slice(2 * a, 2 * a + 2)
-                nc.vector.scalar_tensor_tensor(o[:, pr, :], hp[u][:, pr, :], 0.5, hi2[:, pr, :], ALU.mult, ALU.add)
-                nc.sync.dma_start(out_v[:, pr, cols], o[:, pr, :])
-            if u == 0:
-                interleave(nc.scalar.copy, o_bf[:], o[:])
-            else:
-                interleave(nc.scalar.copy, o_bf[:, 0:96, :], o[:, :, 0:96])
-                interleave(nc.vector.tensor_copy, o_bf[:, 96:, :], o[:, :, 96:])
-            nc.vector.quantize_mx(o_codes[:, cols].bitcast(FP8X4), o_sc[:, cols], o_bf[:].rearrange("p c t -> p (c t)"))
+        da = [keep.tile([P, PACK, HALF], F32, name="da%d" % u) for u in range(2)]
+        db = [keep.tile([P, PACK, HALF], F32, name="db%d" % u) for u in range(2)]
+        top = [keep.tile([P, PACK, HALF], F32, name="top%d" % u) for u in range(2)]
+        low = [keep.tile([P, PACK, HALF], F32, name="low%d" % u) for u in range(2)]
+        o = [keep.tile([P, PACK, HALF], F32, name="o%d" % u) for u in range(2)]
+        o_bf = [keep.tile([P, HALF, PACK], BF16, name="o_bf%d" % u, tag="o_bf_place%d" % u, align_bytes=64) for u in range(2)]
+
+        def fetch(u, t):
+            nc.vector.tensor_tensor(da[u][:, t, :], h_win[t][:].indirect(entries(n3_sb, u * HALF, HALF)), h_neg[u][:, t, :], ALU.add)
+            nc.vector.tensor_tensor(db[u][:, t, :], h_win[t][:].indirect(entries(n4_sb, u * HALF, HALF)), h_neg[u][:, t, :], ALU.add)
+
+        def extremes(u, ts):
+            nc.vector.scalar_tensor_tensor(top[u][:, ts, :], da[u][:, ts, :], 0.0, db[u][:, ts, :], ALU.max, ALU.max)
+            nc.vector.scalar_tensor_tensor(low[u][:, ts, :], da[u][:, ts, :], 0.0, db[u][:, ts, :], ALU.min, ALU.min)
+
+        blocks = [slice(b * P, (b + 1) * P) for b in range(4)]
+
+        def sum_turned(dst_ps, terms):
+            for k, term in enumerate(terms):
+                for b, cols in enumerate(blocks):
+                    first, last = k == 0 and b == 0, k == len(terms) - 1 and b == len(blocks) - 1
+                    nc.tensor.matmul(dst_ps[:, cols], lhsT=term[:, cols], rhs=ident[:], start=first, stop=last, is_transpose=True)
+
+        def finish_on_tensor(u, pair, top_ps, low_ps, back_ps):
+            ts = slice(2 * pair, 2 * pair + 2)
+            extremes(u, ts)
+            top_t = keep.tile([P, 2 * HALF], F32, name="top_t%d" % (2 * u + pair))
+            low_t = keep.tile([P, 2 * HALF], F32, name="low_t%d" % (2 * u + pair))
+            flat = [x[u][:, ts, :].rearrange("p t c -> p (t c)") for x in (top, h_neg, low)]
+            sum_turned(top_ps, flat[0:1])
+            nc.scalar.copy(top_t[:], top_ps[:])
+            sum_turned(low_ps, flat[1:3])
+            nc.scalar.activation(low_t[:], low_ps[:], ACT.Copy, scale=-0.5)
+            sum_turned(back_ps, [top_t, low_t])
+            nc.scalar.copy(o[u][:, ts, :].rearrange("p t c -> p (t c)"), back_ps[:])
+            nc.scalar.dma_start(out_v[:, ts, u * HALF : (u + 1) * HALF], o[u][:, ts, :])
+            nc.scalar.copy(o_bf[u][:, :, ts], back_ps[:].rearrange("p (t c) -> p c t", t=2))
+
+        def hand_out(u):
+            cols = slice(u * HALF, (u + 1) * HALF)
+            nc.vector.quantize_mx(o_codes[:, cols].bitcast(FP8X4), o_sc[:, cols], o_bf[u][:].rearrange("p c t -> p (c t)"))
             nc.sync.dma_start(words_v[:, cols], o_codes[:, cols])
+
+        units = [(0, 0), (0, 1), (1, 0), (1, 1)]
+        for k, (u, pair) in enumerate(units):
+            if k > 0:
+                finish_on_tensor(units[k - 1][0], units[k - 1][1], bank[(0, 1, 0)[k - 1]], bank[(1, 0, 1)[k - 1]], bank[(2, 3, 2)[k - 1]])
+            fetch(u, 2 * pair)
+            fetch(u, 2 * pair + 1)
+        hand_out(0)
+        aux = keep.tile([P, 2, HALF], F32, name="aux", tag="o_bf_place0", align_bytes=64)
+        rear = slice(2, 4)
+        for c in quarters:
+            nc.vector.scalar_tensor_tensor(top[1][:, rear, c], da[1][:, rear, c], 0.0, db[1][:, rear, c], ALU.max, ALU.max)
+            nc.vector.scalar_tensor_tensor(low[1][:, rear, c], da[1][:, rear, c], 0.0, db[1][:, rear, c], ALU.min, ALU.min)
+        for c in quarters:
+            nc.vector.scalar_tensor_tensor(aux[:, :, c], low[1][:, rear, c], -0.5, top[1][:, rear, c], ALU.mult, ALU.add)
+        for c in quarters:
+            nc.vector.scalar_tensor_tensor(o[1][:, rear, c], h_neg[1][:, rear, c], -0.5, aux[:, :, c], ALU.mult, ALU.add)
+        nc.sync.dma_start(out_v[:, rear, HALF:], o[1][:, rear, :])
+        for c in quarters:
+            nc.vector.tensor_copy(o_bf[1][:, c, rear], o[1][:, rear, c].rearrange("p t c -> p c t"))
+        for c in quarters:
+            cols = slice(HALF + c.start, HALF + c.stop)
+            nc.vector.quantize_mx(o_codes[:, cols].bitcast(FP8X4), o_sc[:, cols], o_bf[1][:, c, :].rearrange("p c t -> p (c t)"))
+        nc.sync.dma_start(words_v[:, HALF:], o_codes[:, HALF:])
         for q in range(4):
             eng = nc.scalar if q % 2 == 0 else nc.sync
             eng.dma_start(out_2[0, 4 * q : 4 * q + 4, :].bitcast(I32), o_sc[32 * q : 32 * q + 4, :].bitcast(I32))

from contextlib import ExitStack

import concourse.mybir as mybir
from concourse.masks import make_identity

K, T, S, N, H = 512, 2048, 512, 512, 512
FLOPS = 2 * K * S * H + 2 * S * N * H

F32 = mybir.dt.float32
BF16 = mybir.dt.bfloat16
I32 = mybir.dt.int32
U32 = mybir.dt.uint32
U16 = mybir.dt.uint16
U8 = mybir.dt.uint8
FP8X4 = mybir.dt.float8_e4m3fn_x4
FP4X4 = mybir.dt.float4_e2m1fn_x4
ALU = mybir.AluOpType
ACT = mybir.ActivationFunctionType

P = 128
PACK = 4
HALF = H // 2


def interleave(engine_copy, dst, src):
    engine_copy(dst.rearrange("p (c i) t -> p c t i", i=4), src.rearrange("p t (c i) -> p c t i", i=4))


def entries(offsets, lo, width):
    return offsets[:, lo // 16 : (lo + width) // 16]


def tile_picked_tokhopprange_none_po_kernel(tc, x_words, x_scales, wa, gt, w1_words, w1_scales, offs, n1, n2, n3, n4, out_0, out_1, out_2):
    nc = tc.nc
    with ExitStack() as ctx:
        lists = ctx.enter_context(tc.tile_pool(name="lists", bufs=1))
        keep = ctx.enter_context(tc.tile_pool(name="keep", bufs=1))
        psum = ctx.enter_context(tc.psum_pool(name="psum", bufs=1))

        offs_sb = lists.tile([P, S // 16], U16, name="offs_sb")
        n1_sb = lists.tile([P, H // 16], U16, name="n1_sb")
        n2_sb = lists.tile([P, H // 16], U16, name="n2_sb")
        n3_sb = lists.tile([P, H // 16], U16, name="n3_sb")
        n4_sb = lists.tile([P, H // 16], U16, name="n4_sb")
        bank = [psum.tile([P, H], F32, name="bank%d" % b) for b in range(8)]

        ident = keep.tile([P, P], F32, name="ident")
        xs_tab = keep.tile([P, T], U8, name="xs_tab", tag="xs_place", align_bytes=64)
        wa_raw = keep.tile([P, PACK, H], F32, name="wa_raw")
        gt_sb = keep.tile([P, PACK], F32, name="gt_sb")
        y_win = [keep.tile([P, 2 * H], F32, name="y_win%d" % t, align_bytes=64) for t in range(PACK)]
        warm = keep.tile([P, 8], F32, name="warm", tag="x_place", align_bytes=64)

        nc.sync.dma_start(offs_sb[:], offs)
        nc.sync.dma_start(gt_sb[:], gt.rearrange("(p t) o -> p (t o)", t=PACK))
        nc.vector.memset(xs_tab[:].bitcast(I32), 0)
        nc.vector.memset(warm[:, 0:4], 0.0)
        nc.scalar.activation(warm[:, 4:8], warm[:, 0:4], ACT.Tanh)
        for t in range(PACK):
            nc.vector.memset(y_win[t][:, H:], 0.0)
        th_win = [keep.tile([P, 2 * H if t == PACK - 1 else H], F32, name="th_win%d" % t, align_bytes=64) for t in range(PACK)]
        nc.vector.memset(th_win[PACK - 1][:, H:], 0.0)
        make_identity(nc, ident[:])

        gt_safe = keep.tile([P, PACK], F32, name="gt_safe", tag="w1w_place", align_bytes=64)
        gt_rec = keep.tile([P, PACK], F32, name="gt_rec", tag="w1s_place", align_bytes=64)
        gt_inv = keep.tile([P, PACK], F32, name="gt_inv")
        nc.vector.scalar_tensor_tensor(gt_safe[:], gt_sb[:], 0.0, gt_sb[:], ALU.is_equal, ALU.add)
        nc.vector.reciprocal(gt_rec[:], gt_safe[:])
        nc.vector.tensor_scalar(gt_inv[:], gt_rec[:], 1.0e38, -1.0e38, ALU.min, ALU.max)

        xw_tab = keep.tile([P, T], I32, name="xw_tab", tag="x_place", align_bytes=64)
        w1w_raw = keep.tile([P, 2 * N], U8, name="w1w_raw", tag="w1w_place", align_bytes=64)
        w1s_raw = keep.tile([P, N], U8, name="w1s_raw", tag="w1s_place", align_bytes=64)
        nc.vector.memset(w1s_raw[:].bitcast(I32), 0)

        nc.sync.dma_start(n1_sb[:], n1)
        nc.sync.dma_start(n2_sb[:], n2)
        nc.sync.dma_start(wa_raw[:], wa.rearrange("(p j) c -> p j c", j=PACK))
        for q in range(4):
            nc.sync.dma_start(xs_tab[32 * q : 32 * q + 4, :].bitcast(I32), x_scales[0, 4 * q : 4 * q + 4, :].bitcast(I32))
        nc.sync.dma_start(xw_tab[:], x_words[0].rearrange("p n t -> p (n t)").bitcast(I32))
        nc.sync.dma_start(n3_sb[:], n3)
        nc.sync.dma_start(n4_sb[:], n4)
        nc.sync.dma_start(w1w_raw[:].bitcast(I32), w1_words[0].bitcast(I32))
        for q in range(4):
            nc.sync.dma_start(w1s_raw[32 * q : 32 * q + 4, :].bitcast(I32), w1_scales[0, 4 * q : 4 * q + 4, :].bitcast(I32))

        wa_bf = [keep.tile([P, HALF, PACK], BF16, name="wa_bf%d" % u, align_bytes=64) for u in range(2)]
        wa_codes = keep.tile([P, H], U32, name="wa_codes", align_bytes=64)
        xs_pick = keep.tile([P, S], U8, name="xs_pick", tag="xw_place", align_bytes=64)
        xs = keep.tile([P, S], U8, name="xs", align_bytes=64)
        halves = [slice(0, HALF), slice(HALF, H)]
        interleave(nc.vector.tensor_copy, wa_bf[1][:, HALF - 128 :, :], wa_raw[:, :, H - 128 :])
        interleave(nc.scalar.copy, wa_bf[0][:], wa_raw[:, :, halves[0]])
        interleave(nc.scalar.copy, wa_bf[1][:, 0 : HALF - 128, :], wa_raw[:, :, HALF : H - 128])
        nc.vector.tensor_copy(xs_pick[:], xs_tab[:].indirect(offs_sb[:]))
        wa_sc = keep.tile([P, H], U8, name="wa_sc", tag="xs_place", align_bytes=64)
        nc.vector.quantize_mx(wa_codes[:, halves[0]].bitcast(FP8X4), wa_sc[:, halves[0]], wa_bf[0][:].rearrange("p c t -> p (c t)"))
        nc.vector.tensor_copy(xs[:].rearrange("p (t m) -> p t m", t=PACK), xs_pick[:].rearrange("p (m t) -> p t m", t=PACK))
        xw = keep.tile([P, S], U32, name="xw", tag="xw_place", align_bytes=64)
        nc.vector.tensor_copy(xw[:].rearrange("p (t m) -> p m t", t=PACK), xw_tab[:].bitcast(U32).indirect(offs_sb[:]))
        nc.vector.quantize_mx(wa_codes[:, halves[1]].bitcast(FP8X4), wa_sc[:, halves[1]], wa_bf[1][:].rearrange("p c t -> p (c t)"))

        y_plain = [keep.tile([P, H], F32, name="y_plain%d" % t) for t in range(PACK)]
        for t in range(PACK):
            m = slice(t * P, (t + 1) * P)
            g = gt_sb[:, t : t + 1]
            if t == 0:
                for u in range(2):
                    cols = slice(u * HALF, (u + 1) * HALF)
                    nc.tensor.matmul_mx(bank[4 * u][:, 0:HALF], lhsT=xw[:, m].bitcast(FP8X4), lhsT_scale=xs[:, m], rhs=wa_codes[:, cols].bitcast(FP8X4), rhs_scale=wa_sc[:, cols], start=True, stop=True)
                nc.scalar.activation(y_win[t][:, 0:HALF], bank[0][:, 0:HALF], ACT.Copy, scale=g)
                nc.scalar.activation(y_win[t][:, HALF:H], bank[4][:, 0:HALF], ACT.Copy, scale=g)
                nc.vector.tensor_scalar(y_plain[t][:, 0:HALF], bank[0][:, 0:HALF], g, None, ALU.mult)
                nc.scalar.activation(y_plain[t][:, HALF:H], bank[4][:, 0:HALF], ACT.Copy, scale=g)
            else:
                nc.tensor.matmul_mx(bank[t][:], lhsT=xw[:, m].bitcast(FP8X4), lhsT_scale=xs[:, m], rhs=wa_codes[:].bitcast(FP8X4), rhs_scale=wa_sc[:], start=True, stop=True)
                nc.scalar.activation(y_win[t][:, 0:H], bank[t][:], ACT.Copy, scale=g)
                nc.scalar.activation(y_plain[t][:], bank[t][:], ACT.Copy, scale=g)

        w1w = keep.tile([P, 2 * N], U8, name="w1w", tag="x_place", align_bytes=64)
        w1s = keep.tile([P, N], U8, name="w1s", tag="w1w_place", align_bytes=64)
        nc.vector.tensor_copy(w1w[:].rearrange("p (t m b) -> p t m b", t=PACK, b=2), w1w_raw[:].rearrange("p (m t b) -> p t m b", t=PACK, b=2))
        nc.vector.tensor_copy(w1s[:].rearrange("p (t m) -> p t m", t=PACK), w1s_raw[:].rearrange("p (m t) -> p t m", t=PACK))

        stg = keep.tile([P, PACK, H], F32, name="stg")
        for t in range(PACK):
            nc.vector.tensor_tensor(stg[:, PACK - 1 - t, :], y_win[t][:].indirect(n1_sb[:]), y_plain[t][:], ALU.add)
            nc.scalar.activation(th_win[t][:, 0:H], stg[:, PACK - 1 - t, :], ACT.Tanh, scale=gt_inv[:, t : t + 1])

        h_win = [keep.tile([P, H], F32, name="h_win%d" % t, align_bytes=64) for t in range(PACK)]
        h_neg = [keep.tile([P, PACK, HALF], F32, name="h_neg%d" % u) for u in range(2)]
        z_left = keep.tile([P, PACK, HALF], F32, name="z_left")
        z_pair = [th_win[PACK - 1][:, H:].rearrange("p (t c) -> p t c", t=2), stg[:, 0:2, 0:HALF]]
        z_bf = [keep.tile([P, HALF, PACK], BF16, name="z_bf%d" % u, align_bytes=64) for u in range(2)]
        z_codes = [keep.tile([P, HALF], U32, name="z_codes%d" % u, align_bytes=64) for u in range(2)]
        z_sc = [keep.tile([P, HALF], U8, name="z_sc%d" % u, align_bytes=64) for u in range(2)]
        quarters = [slice(0, P), slice(P, HALF)]
        for t in range(PACK):
            nc.vector.tensor_tensor(z_left[:, t, :], th_win[t][:].indirect(entries(n2_sb, 0, HALF)), stg[:, PACK - 1 - t, 0:HALF], ALU.mult)
        interleave(nc.scalar.copy, z_bf[0][:], z_left[:])
        for t in range(PACK):
            nc.vector.tensor_tensor(z_pair[t // 2][:, t % 2, :], th_win[t][:].indirect(entries(n2_sb, HALF, HALF)), stg[:, PACK - 1 - t, HALF:], ALU.mult)
        nc.scalar.copy(z_bf[1][:, :, 0:2], z_pair[0].rearrange("p t c -> p c t"))
        nc.vector.quantize_mx(z_codes[0][:].bitcast(FP8X4), z_sc[0][:], z_bf[0][:].rearrange("p c t -> p (c t)"))
        for c in quarters:
            nc.vector.tensor_copy(z_bf[1][:, c, 2:4], z_pair[1][:, :, c].rearrange("p t c -> p c t"))
        for c in quarters:
            nc.vector.quantize_mx(z_codes[1][:, c].bitcast(FP8X4), z_sc[1][:, c], z_bf[1][:, c, :].rearrange("p c t -> p (c t)"))

        def second_product(t, u, c):
            nc.tensor.matmul_mx(bank[PACK * u + t][:, c], lhsT=w1w[:, 2 * P * t : 2 * P * (t + 1)].bitcast(FP4X4), lhsT_scale=w1s[:, t * P : (t + 1) * P], rhs=z_codes[u][:, c].bitcast(FP8X4), rhs_scale=z_sc[u][:, c], start=True, stop=True)

        for t in range(PACK):
            second_product(t, 0, slice(0, HALF))
            for c in quarters if t == 0 else [slice(0, HALF)]:
                second_product(t, 1, c)
            nc.scalar.copy(h_win[t][:, 0:HALF], bank[t][:, 0:HALF])
            nc.scalar.activation(h_neg[0][:, t, :], bank[t][:, 0:HALF], ACT.Copy, scale=-1.0)
            nc.scalar.copy(h_win[t][:, HALF:H], bank[PACK + t][:, 0:HALF])
        for t in range(PACK):
            nc.scalar.activation(h_neg[1][:, t, :], bank[PACK + t][:, 0:HALF], ACT.Copy, scale=-1.0)

        o_codes = keep.tile([P, H], I32, name="o_codes", align_bytes=64)
        o_sc = keep.tile([P, H], U8, name="o_sc", align_bytes=64)
        out_v = out_0.rearrange("(p t) c -> p t c", t=PACK)
        words_v = out_1[0].rearrange("p n t -> p (n t)").bitcast(I32)
        da = [keep.tile([P, PACK, HALF], F32, name="da%d" % u) for u in range(2)]
        db = [keep.tile([P, PACK, HALF], F32, name="db%d" % u) for u in range(2)]
        top = [keep.tile([P, PACK, HALF], F32, name="top%d" % u) for u in range(2)]
        low = [keep.tile([P, PACK, HALF], F32, name="low%d" % u) for u in range(2)]
        o = [keep.tile([P, PACK, HALF], F32, name="o%d" % u) for u in range(2)]
        o_bf = [keep.tile([P, HALF, PACK], BF16, name="o_bf%d" % u, tag="o_bf_place%d" % u, align_bytes=64) for u in range(2)]

        def fetch(u, t):
            nc.vector.tensor_tensor(da[u][:, t, :], h_win[t][:].indirect(entries(n3_sb, u * HALF, HALF)), h_neg[u][:, t, :], ALU.add)
            nc.vector.tensor_tensor(db[u][:, t, :], h_win[t][:].indirect(entries(n4_sb, u * HALF, HALF)), h_neg[u][:, t, :], ALU.add)

        def extremes(u, ts):
            nc.vector.scalar_tensor_tensor(top[u][:, ts, :], da[u][:, ts, :], 0.0, db[u][:, ts, :], ALU.max, ALU.max)
            nc.vector.scalar_tensor_tensor(low[u][:, ts, :], da[u][:, ts, :], 0.0, db[u][:, ts, :], ALU.min, ALU.min)

        blocks = [slice(b * P, (b + 1) * P) for b in range(4)]

        def sum_turned(dst_ps, terms):
            for k, term in enumerate(terms):
                for b, cols in enumerate(blocks):
                    first, last = k == 0 and b == 0, k == len(terms) - 1 and b == len(blocks) - 1
                    nc.tensor.matmul(dst_ps[:, cols], lhsT=term[:, cols], rhs=ident[:], start=first, stop=last, is_transpose=True)

        def finish_on_tensor(u, pair, top_ps, low_ps, back_ps):
            ts = slice(2 * pair, 2 * pair + 2)
            extremes(u, ts)
            top_t = keep.tile([P, 2 * HALF], F32, name="top_t%d" % (2 * u + pair))
            low_t = keep.tile([P, 2 * HALF], F32, name="low_t%d" % (2 * u + pair))
            flat = [x[u][:, ts, :].rearrange("p t c -> p (t c)") for x in (top, h_neg, low)]
            sum_turned(top_ps, flat[0:1])
            nc.scalar.copy(top_t[:], top_ps[:])
            sum_turned(low_ps, flat[1:3])
            nc.scalar.activation(low_t[:], low_ps[:], ACT.Copy, scale=-0.5)
            sum_turned(back_ps, [top_t, low_t])
            nc.scalar.copy(o[u][:, ts, :].rearrange("p t c -> p (t c)"), back_ps[:])
            nc.scalar.dma_start(out_v[:, ts, u * HALF : (u + 1) * HALF], o[u][:, ts, :])
            nc.scalar.copy(o_bf[u][:, :, ts], back_ps[:].rearrange("p (t c) -> p c t", t=2))

        def hand_out(u):
            cols = slice(u * HALF, (u + 1) * HALF)
            nc.vector.quantize_mx(o_codes[:, cols].bitcast(FP8X4), o_sc[:, cols], o_bf[u][:].rearrange("p c t -> p (c t)"))
            nc.sync.dma_start(words_v[:, cols], o_codes[:, cols])

        units = [(0, 0), (0, 1), (1, 0), (1, 1)]
        for k, (u, pair) in enumerate(units):
            if k > 0:
                finish_on_tensor(units[k - 1][0], units[k - 1][1], bank[(0, 1, 0)[k - 1]], bank[(1, 0, 1)[k - 1]], bank[(2, 3, 2)[k - 1]])
            fetch(u, 2 * pair)
            fetch(u, 2 * pair + 1)
        hand_out(0)
        aux = keep.tile([P, 2, HALF], F32, name="aux", tag="o_bf_place0", align_bytes=64)
        rear = slice(2, 4)
        for c in quarters:
            nc.vector.scalar_tensor_tensor(top[1][:, rear, c], da[1][:, rear, c], 0.0, db[1][:, rear, c], ALU.max, ALU.max)
            nc.vector.scalar_tensor_tensor(low[1][:, rear, c], da[1][:, rear, c], 0.0, db[1][:, rear, c], ALU.min, ALU.min)
        for c in quarters:
            nc.vector.scalar_tensor_tensor(aux[:, :, c], low[1][:, rear, c], -0.5, top[1][:, rear, c], ALU.mult, ALU.add)
        for c in quarters:
            nc.vector.scalar_tensor_tensor(o[1][:, rear, c], h_neg[1][:, rear, c], -0.5, aux[:, :, c], ALU.mult, ALU.add)
        nc.sync.dma_start(out_v[:, rear, HALF:], o[1][:, rear, :])
        for c in quarters:
            nc.vector.tensor_copy(o_bf[1][:, c, rear], o[1][:, rear, c].rearrange("p t c -> p c t"))
        for c in quarters:
            cols = slice(HALF + c.start, HALF + c.stop)
            nc.vector.quantize_mx(o_codes[:, cols].bitcast(FP8X4), o_sc[:, cols], o_bf[1][:, c, :].rearrange("p c t -> p (c t)"))
        nc.sync.dma_start(words_v[:, HALF:], o_codes[:, HALF:])
        for q in range(4):
            eng = nc.scalar if q % 2 == 0 else nc.sync
            eng.dma_start(out_2[0, 4 * q : 4 * q + 4, :].bitcast(I32), o_sc[32 * q : 32 * q + 4, :].bitcast(I32))
